import numpy as np
import ml_dtypes


def mxq(x, axis, fmt="e4m3"):
    dtype, down = {"e4m3": (ml_dtypes.float8_e4m3fn, 7), "e5m2": (ml_dtypes.float8_e5m2, 14)}[fmt]
    v = np.moveaxis(np.asarray(x, np.float32).astype(ml_dtypes.bfloat16).astype(np.float64), axis, -1)
    blocks = v.reshape(v.shape[:-1] + (-1, 32))
    amax = np.abs(blocks).max(-1, keepdims=True)
    byte = np.maximum(np.where(amax > 0, np.frexp(amax)[1] - 1 + 127, 0) - down, 1)
    scale = np.exp2(byte - 127.0)
    codes = (blocks / scale).astype(np.float32).astype(dtype).astype(np.float64)
    return np.moveaxis((codes * scale).reshape(v.shape), -1, axis)


WIDE = False


def mx_kscale(k):
    if not WIDE:
        return np.ones(k)
    levels = np.array([10, -10, 5, -5, 0])
    if k % 512:
        return np.exp2(np.random.permutation(np.resize(levels, k // 32))).repeat(32)
    a = np.empty((k // 512, 16))
    for p in range(k // 512):
        a[p, :8] = np.random.permutation(np.resize(levels, 8))
        for g in range(8):
            far = levels[np.abs(levels - a[p, g]) >= 10]
            a[p, g + 8] = far[np.random.randint(len(far))]
    return np.exp2(a.ravel()).repeat(32)


BF16 = ml_dtypes.bfloat16


def bf(x):
    return np.asarray(x, np.float32).astype(BF16)


def f64(x):
    return np.asarray(x).astype(np.float64)


E2M1 = np.array([0.0, 0.5, 1.0, 1.5, 2.0, 3.0, 4.0, 6.0, -0.0, -0.5, -1.0, -1.5, -2.0, -3.0, -4.0, -6.0])


def pack_weight(w, fmt):
    k, n = w.shape
    w = f64(bf(w)).reshape(k // 32, 32, n)
    amax = np.abs(w).max(1)
    if fmt == "e4m3":
        byte = np.frexp(amax)[1] - 1 + 127 - 7
    else:
        mant, ex = np.frexp(amax / 6.0)
        byte = np.where(mant > 0.5, ex, ex - 1) + 127
    byte = np.clip(np.where(amax > 0, byte, 1), 1, 254)
    scaled = (w * np.exp2(127.0 - byte)[:, None, :]).reshape(k, n).astype(np.float32)
    by_word = np.ascontiguousarray(scaled.reshape(k // 512, 128, 4, n).transpose(0, 1, 3, 2))
    if fmt == "e4m3":
        words = by_word.astype(ml_dtypes.float8_e4m3fn).view(np.uint8)
    else:
        c = by_word.astype(ml_dtypes.float4_e2m1fn).view(np.uint8) & 0xF
        words = c[..., 0::2] | (c[..., 1::2] << 4)
    return np.ascontiguousarray(words), np.ascontiguousarray(byte.astype(np.uint8).reshape(k // 512, 16, n))


def unpack_weight(words, scales, fmt):
    g, p, n, _ = words.shape
    if fmt == "e4m3":
        vals = np.ascontiguousarray(words).view(ml_dtypes.float8_e4m3fn).astype(np.float64)
    else:
        nib = np.empty((g, p, n, 4), np.uint8)
        nib[..., 0::2] = words & 0xF
        nib[..., 1::2] = words >> 4
        vals = E2M1[nib]
    vals = vals * np.repeat(np.exp2(scales.astype(np.float64) - 127.0), 8, axis=1)[..., None]
    return vals.transpose(0, 1, 3, 2).reshape(g * 512, n)
def pack4(w):
    words, scales = pack_weight(w, "e2m1")
    return words.reshape(words.shape[0], 128, -1), scales


def unpack4(words, scales):
    return unpack_weight(words.reshape(words.shape[0], 128, -1, 2), scales, "e2m1")


T, D, E, V = 512, 2048, 1024, 2560

CAP = 4.0


def setup_inputs():
    s = mx_kscale(D)
    u = mx_kscale(E)
    hidden = np.random.standard_normal((T, D)) * s
    emb = np.random.standard_normal((T, E)) * u
    vh = np.random.standard_normal((D, V)) / np.sqrt(D) / s[:, None]
    ve = np.random.standard_normal((E, V)) / np.sqrt(E) / u[:, None]
    vh_words, vh_scales = pack4(vh)
    return {"hidden": bf(hidden),
            "emb": bf(emb),
            "vh_words": vh_words,
            "vh_scales": vh_scales,
            "ve": bf(ve),
            "bias": bf(0.3 * np.random.standard_normal(V))}


def reference(hidden, emb, vh_words, vh_scales, ve, bias):
    vh = unpack4(vh_words, vh_scales)
    hq = mxq(f64(hidden), 1, "e4m3")
    eq = mxq(f64(emb), 1, "e4m3")
    vq = mxq(f64(ve), 0, "e4m3")
    z = (hq @ vh) + (eq @ vq)
    z = z + f64(bias)
    return CAP * np.tanh(z / CAP)

@@ -1,0 +1,273 @@
+from contextlib import ExitStack
+
+import concourse.mybir as mybir
+from concourse.masks import make_identity
+
+T, D, E, V = 512, 2048, 1024, 2560
+CAP = 4.0
+FLOPS = 2 * T * (D + E) * V
+
+F32 = mybir.dt.float32
+BF16 = mybir.dt.bfloat16
+I32 = mybir.dt.int32
+U32 = mybir.dt.uint32
+U8 = mybir.dt.uint8
+FP8X4 = mybir.dt.float8_e4m3fn_x4
+FP4X4 = mybir.dt.float4_e2m1fn_x4
+ALU = mybir.AluOpType
+ACT = mybir.ActivationFunctionType
+
+P = 128
+PACK = 4
+K_PASS = P * PACK
+N_TILE = 512
+M_TILES = T // P
+N_TILES = V // N_TILE
+H_PASSES = D // K_PASS
+E_PASSES = E // K_PASS
+PART = 2 * K_PASS
+N_GROUPS = ((0,), (1, 2), (3, 4))
+BANKS = 8
+
+
+def tile_multi_token_draft_logits_s1_kernel(tc, hidden, emb, vh_words, vh_scales, ve, bias, out):
+    nc = tc.nc
+    with ExitStack() as ctx:
+        keep = ctx.enter_context(tc.tile_pool(name="keep", bufs=1))
+        stage = ctx.enter_context(tc.tile_pool(name="stage", bufs=4))
+        psum = ctx.enter_context(tc.psum_pool(name="psum", bufs=1))
+        ctx.enter_context(tc.manual_schedule())
+
+        def bank(b):
+            return psum.tile([P, N_TILE], F32, name="bank%d" % b, tag="bank%d" % b)
+
+        x_raw = {}
+        vh_w, vh_s, ve_raw = {}, {}, {}
+        for gi, group in enumerate(N_GROUPS):
+            width = N_TILE * len(group)
+            vh_w[gi] = keep.tile([P, H_PASSES, 2 * width], U8, name="vh_w%d" % gi, align_bytes=64)
+            vh_s[gi] = keep.tile([P, H_PASSES, width], U8, name="vh_s%d" % gi, align_bytes=64)
+            for g in range(E_PASSES):
+                ve_raw[gi, g] = keep.tile([P, PACK, width], BF16, name="ve_raw%d_%d" % (gi, g), align_bytes=64)
+        place = {n: (gi, j) for gi, group in enumerate(N_GROUPS) for j, n in enumerate(group)}
+
+        ident = keep.tile([P, P], F32, name="ident")
+        make_identity(nc, ident[:])
+        bias_cols = keep.tile([P, N_TILES * 16], BF16, name="bias_cols")
+        nc.scalar.dma_start(
+            out=bias_cols[:].rearrange("p (n c) -> p n c", c=16)[:, :, 0:PACK],
+            in_=bias.rearrange("(n p t) -> p n t", p=P, t=PACK),
+        )
+        warm = keep.tile([P, 2], F32, name="warm")
+        nc.vector.memset(warm[:, 0:1], 0.0)
+        nc.scalar.activation(out=warm[:, 1:2], in_=warm[:, 0:1], func=ACT.Tanh)
+        for gi in range(len(N_GROUPS)):
+            nc.vector.memset(vh_s[gi][:].rearrange("p g n -> p (g n)").bitcast(I32), 0)
+
+        def load_x(src, m, first_part, parts, col0):
+            raw = keep.tile([P, parts * PART], BF16, name="x_raw%d_%d" % (m, first_part), align_bytes=64)
+            nc.sync.dma_start(out=raw[:], in_=src[m * P:(m + 1) * P, col0:col0 + parts * PART])
+            for i in range(parts):
+                x_raw[m, first_part + i] = raw[:, i * PART:(i + 1) * PART]
+
+        def group_cols(gi):
+            return N_GROUPS[gi][0] * N_TILE, (N_GROUPS[gi][-1] + 1) * N_TILE
+
+        def load_vh(gi):
+            c0, c1 = group_cols(gi)
+            for r in range(4):
+                nc.sync.dma_start(
+                    out=vh_s[gi][r:P:32, :, :].bitcast(I32),
+                    in_=vh_scales[:, r:16:4, c0:c1].rearrange("g q n -> q g n").bitcast(I32),
+                )
+            nc.sync.dma_start(
+                out=vh_w[gi][:].bitcast(I32),
+                in_=vh_words[:, :, 2 * c0:2 * c1].rearrange("g p b -> p g b").bitcast(I32),
+            )
+
+        def load_ve(gi, g):
+            c0, c1 = group_cols(gi)
+            nc.sync.dma_start(
+                out=ve_raw[gi, g][:],
+                in_=ve[g * K_PASS:(g + 1) * K_PASS, c0:c1].rearrange("(p j) w -> p j w", j=PACK),
+            )
+
+        load_x(hidden, 0, 0, 1, 0)
+        load_x(hidden, 0, 1, 1, PART)
+        load_vh(0)
+        load_x(hidden, 1, 0, 2, 0)
+        load_x(hidden, 2, 0, 2, 0)
+        load_ve(0, 0)
+        load_x(hidden, 3, 0, 2, 0)
+        for m in range(M_TILES):
+            load_x(emb, m, 2, 1, 0)
+        load_ve(0, 1)
+        for gi in (1, 2):
+            load_vh(gi)
+            load_ve(gi, 0)
+            load_ve(gi, 1)
+
+        turns = []
+        x_grouped, x_codes, x_scales = {}, {}, {}
+
+        def next_turn_bank():
+            b = 4 + len(turns) % 4
+            turns.append(b)
+            return bank(b)
+
+        def unpack_words(copy, dst, src, groups):
+            copy(
+                out=dst.bitcast(F32).rearrange("p (g r u) -> p g r u", g=groups, u=2),
+                in_=src.rearrange("p (g u r) -> p g r u", g=groups, u=2),
+            )
+
+        def transpose_x(m, part):
+            words = x_raw[m, part].bitcast(F32)
+            turned = next_turn_bank()
+            for g in range(2):
+                for u in range(2):
+                    col = (2 * g + u) * P
+                    nc.tensor.transpose(turned[:, col:col + P], words[:, 256 * g + u:256 * (g + 1):2], ident[:])
+            grouped = stage.tile([P, PART], BF16, name="x_grouped", align_bytes=64)
+            unpack_words(nc.scalar.copy, grouped[:], turned[:], 2)
+            x_grouped[m, part] = grouped
+
+        def quantize_x(m, part):
+            codes = keep.tile([P, 2 * P], U32, name="x_codes%d_%d" % (m, part), align_bytes=64)
+            scales = keep.tile([P, 2 * P], U8, name="x_scales%d_%d" % (m, part), align_bytes=64)
+            nc.vector.quantize_mx(out=codes[:].bitcast(FP8X4), scales=scales[:], in_=x_grouped[m, part][:])
+            x_codes[m, part], x_scales[m, part] = codes, scales
+
+        bias_rows = keep.tile([P, V], BF16, name="bias_rows")
+        bias_banks = []
+
+        def transpose_bias():
+            words = bias_cols[:].bitcast(F32)
+            for n0 in range(0, N_TILES, 2):
+                tiles = min(2, N_TILES - n0)
+                turned = next_turn_bank()
+                for i in range(tiles):
+                    for u in range(2):
+                        col = (2 * i + u) * P
+                        word = (n0 + i) * 8 + u
+                        nc.tensor.transpose(
+                            turned[:, col:col + P], words[:, word:word + 1].to_broadcast([P, P]), ident[:]
+                        )
+                bias_banks.append((n0, tiles, turned))
+
+        def copy_bias():
+            for n0, tiles, turned in bias_banks:
+                unpack_words(
+                    nc.vector.tensor_copy,
+                    bias_rows[:, n0 * N_TILE:(n0 + tiles) * N_TILE],
+                    turned[:, 0:tiles * 2 * P],
+                    tiles,
+                )
+
+        ve_grouped, ve_codes, ve_scales = {}, {}, {}
+
+        def interleave_ve(n, g, scalar_cols=0):
+            gi, j = place[n]
+            grouped = stage.tile([P, N_TILE, PACK], BF16, name="ve_grouped", align_bytes=64, bufs=3)
+            src = ve_raw[gi, g][:, :, j * N_TILE:(j + 1) * N_TILE].rearrange("p j w -> p w j")
+            if scalar_cols:
+                nc.scalar.copy(out=grouped[:, 0:scalar_cols, :], in_=src[:, 0:scalar_cols, :])
+            nc.vector.tensor_copy(out=grouped[:, scalar_cols:, :], in_=src[:, scalar_cols:, :])
+            ve_grouped[n, g] = grouped
+
+        def quantize_ve(n, g):
+            codes = keep.tile([P, N_TILE], U32, name="ve_codes%d_%d" % (n, g), align_bytes=64)
+            scales = keep.tile([P, N_TILE], U8, name="ve_scales%d_%d" % (n, g), align_bytes=64)
+            nc.vector.quantize_mx(
+                out=codes[:].bitcast(FP8X4), scales=scales[:], in_=ve_grouped[n, g][:].rearrange("p w j -> p (w j)")
+            )
+            ve_codes[n, g], ve_scales[n, g] = codes, scales
+
+        acc, logits = {}, {}
+
+        def hidden_passes(m, n):
+            gi, j = place[n]
+            acc[m, n] = bank((4 * n + m) % BANKS)
+            for g in range(H_PASSES):
+                cols = slice((g % 2) * P, (g % 2 + 1) * P)
+                nc.tensor.matmul_mx(
+                    out=acc[m, n][:],
+                    lhsT=x_codes[m, g // 2][:, cols].bitcast(FP8X4),
+                    lhsT_scale=x_scales[m, g // 2][:, cols],
+                    rhs=vh_w[gi][:, g, 2 * j * N_TILE:2 * (j + 1) * N_TILE].bitcast(FP4X4),
+                    rhs_scale=vh_s[gi][:, g, j * N_TILE:(j + 1) * N_TILE],
+                    start=(g == 0),
+                    stop=False,
+                )
+
+        def emb_passes(m, n):
+            for g in range(E_PASSES):
+                cols = slice(g * P, (g + 1) * P)
+                nc.tensor.matmul_mx(
+                    out=acc[m, n][:],
+                    lhsT=x_codes[m, 2][:, cols].bitcast(FP8X4),
+                    lhsT_scale=x_scales[m, 2][:, cols],
+                    rhs=ve_codes[n, g][:].bitcast(FP8X4),
+                    rhs_scale=ve_scales[n, g][:],
+                    start=False,
+                    stop=(g == E_PASSES - 1),
+                )
+
+        def add_bias(m, n):
+            z = keep.tile([P, N_TILE], F32, name="logits%d_%d" % (m, n))
+            nc.vector.tensor_tensor(
+                out=z[:], in0=acc[m, n][:], in1=bias_rows[:, n * N_TILE:(n + 1) * N_TILE], op=ALU.add
+            )
+            nc.scalar.activation(out=z[:], in_=z[:], func=ACT.Tanh, scale=1.0 / CAP)
+            logits[m, n] = z
+
+        def finish(m, n, on_vector):
+            z = logits[m, n]
+            if on_vector:
+                nc.vector.tensor_scalar(out=z[:], in0=z[:], scalar1=CAP, scalar2=None, op0=ALU.mult)
+            else:
+                nc.scalar.activation(out=z[:], in_=z[:], func=ACT.Copy, scale=CAP)
+            nc.sync.dma_start(out=out[m * P:(m + 1) * P, n * N_TILE:(n + 1) * N_TILE], in_=z[:])
+
+        transpose_x(0, 0)
+        transpose_x(0, 1)
+        transpose_bias()
+        quantize_x(0, 0)
+        quantize_x(0, 1)
+        copy_bias()
+        hidden_passes(0, 0)
+        for m in (1, 2):
+            for part in (0, 1):
+                transpose_x(m, part)
+                quantize_x(m, part)
+        hidden_passes(1, 0)
+        interleave_ve(0, 0)
+        for part in (0, 1):
+            transpose_x(3, part)
+            quantize_x(3, part)
+        hidden_passes(2, 0)
+        quantize_ve(0, 0)
+        for m in range(M_TILES):
+            transpose_x(m, 2)
+            quantize_x(m, 2)
+            if m == 1:
+                interleave_ve(0, 1)
+        quantize_ve(0, 1)
+        hidden_passes(3, 0)
+
+        for n in range(N_TILES):
+            more = n + 1 < N_TILES
+            for m in range(M_TILES):
+                if n > 0:
+                    hidden_passes(m, n)
+                emb_passes(m, n)
+                if more and m < 2:
+                    interleave_ve(n + 1, m, scalar_cols=128)
+                add_bias(m, n)
+                if more and m in (1, 2):
+                    quantize_ve(n + 1, m - 1)
+                if more:
+                    finish(m, n, False)
+                elif m > 0:
+                    finish(m - 1, n, True)
+        finish(M_TILES - 1, N_TILES - 1, True)

@@ -26,7 +26,11 @@ N_TILES = V // N_TILE
 H_PASSES = D // K_PASS
 E_PASSES = E // K_PASS
 PART = 2 * K_PASS
-N_GROUPS = ((0,), (1, 2), (3, 4))
+VH_GROUPS = ((0,), (1,), (2,), (3,), (4,))
+VE_GROUPS = ((0,), (1,), (2,), (3,), (4,))
+SC_GROUPS = ((0,), (1,), (2,), (3, 4))
+WARM_PASSES = 8
+SCALAR_COLS = 352
 BANKS = 8
 
 
@@ -38,18 +42,26 @@ def tile_multi_token_draft_logits_s1_kernel(tc, hidden, emb, vh_words, vh_scales
         psum = ctx.enter_context(tc.psum_pool(name="psum", bufs=1))
         ctx.enter_context(tc.manual_schedule())
 
-        def bank(b):
-            return psum.tile([P, N_TILE], F32, name="bank%d" % b, tag="bank%d" % b)
+        free_banks = list(range(BANKS))
+
+        def take_bank():
+            b = free_banks.pop(0)
+            return b, psum.tile([P, N_TILE], F32, name="bank%d" % b, tag="bank%d" % b)
 
         x_raw = {}
         vh_w, vh_s, ve_raw = {}, {}, {}
-        for gi, group in enumerate(N_GROUPS):
-            width = N_TILE * len(group)
-            vh_w[gi] = keep.tile([P, H_PASSES, 2 * width], U8, name="vh_w%d" % gi, align_bytes=64)
-            vh_s[gi] = keep.tile([P, H_PASSES, width], U8, name="vh_s%d" % gi, align_bytes=64)
+        for gi, group in enumerate(VH_GROUPS):
+            vh_w[gi] = keep.tile([P, H_PASSES, 2 * N_TILE * len(group)], U8, name="vh_w%d" % gi, align_bytes=64)
+        for gi, group in enumerate(SC_GROUPS):
+            vh_s[gi] = keep.tile([P, H_PASSES, N_TILE * len(group)], U8, name="vh_s%d" % gi, align_bytes=64)
+        for gi, group in enumerate(VE_GROUPS):
             for g in range(E_PASSES):
-                ve_raw[gi, g] = keep.tile([P, PACK, width], BF16, name="ve_raw%d_%d" % (gi, g), align_bytes=64)
-        place = {n: (gi, j) for gi, group in enumerate(N_GROUPS) for j, n in enumerate(group)}
+                ve_raw[gi, g] = keep.tile(
+                    [P, PACK, N_TILE * len(group)], BF16, name="ve_raw%d_%d" % (gi, g), align_bytes=64
+                )
+
+        def place(groups, n):
+            return [(gi, group.index(n)) for gi, group in enumerate(groups) if n in group][0]
 
         ident = keep.tile([P, P], F32, name="ident")
         make_identity(nc, ident[:])
@@ -58,10 +70,15 @@ def tile_multi_token_draft_logits_s1_kernel(tc, hidden, emb, vh_words, vh_scales
             out=bias_cols[:].rearrange("p (n c) -> p n c", c=16)[:, :, 0:PACK],
             in_=bias.rearrange("(n p t) -> p n t", p=P, t=PACK),
         )
-        warm = keep.tile([P, 2], F32, name="warm")
-        nc.vector.memset(warm[:, 0:1], 0.0)
-        nc.scalar.activation(out=warm[:, 1:2], in_=warm[:, 0:1], func=ACT.Tanh)
-        for gi in range(len(N_GROUPS)):
+        zeros = keep.tile([P, K_PASS], BF16, name="zeros", align_bytes=64)
+        zero_codes = keep.tile([P, P], U32, name="zero_codes", align_bytes=64)
+        zero_scales = keep.tile([P, P], U8, name="zero_scales", align_bytes=64)
+        warm = keep.tile([P, 1], F32, name="warm")
+        nc.vector.memset(zeros[:], 0.0)
+        nc.vector.memset(vh_s[0][:].rearrange("p g n -> p (g n)").bitcast(I32), 0)
+        nc.vector.quantize_mx(out=zero_codes[:].bitcast(FP8X4), scales=zero_scales[:], in_=zeros[:])
+        nc.scalar.activation(out=warm[:], in_=zeros[:, 0:1], func=ACT.Tanh)
+        for gi in range(1, len(SC_GROUPS)):
             nc.vector.memset(vh_s[gi][:].rearrange("p g n -> p (g n)").bitcast(I32), 0)
 
         def load_x(src, m, first_part, parts, col0):
@@ -70,50 +87,60 @@ def tile_multi_token_draft_logits_s1_kernel(tc, hidden, emb, vh_words, vh_scales
             for i in range(parts):
                 x_raw[m, first_part + i] = raw[:, i * PART:(i + 1) * PART]
 
-        def group_cols(gi):
-            return N_GROUPS[gi][0] * N_TILE, (N_GROUPS[gi][-1] + 1) * N_TILE
+        def group_cols(group):
+            return group[0] * N_TILE, (group[-1] + 1) * N_TILE
 
-        def load_vh(gi):
-            c0, c1 = group_cols(gi)
+        def load_sc(gi):
+            c0, c1 = group_cols(SC_GROUPS[gi])
             for r in range(4):
                 nc.sync.dma_start(
                     out=vh_s[gi][r:P:32, :, :].bitcast(I32),
                     in_=vh_scales[:, r:16:4, c0:c1].rearrange("g q n -> q g n").bitcast(I32),
                 )
+
+        def load_vh(gi):
+            c0, c1 = group_cols(VH_GROUPS[gi])
             nc.sync.dma_start(
                 out=vh_w[gi][:].bitcast(I32),
                 in_=vh_words[:, :, 2 * c0:2 * c1].rearrange("g p b -> p g b").bitcast(I32),
             )
 
         def load_ve(gi, g):
-            c0, c1 = group_cols(gi)
+            c0, c1 = group_cols(VE_GROUPS[gi])
             nc.sync.dma_start(
                 out=ve_raw[gi, g][:],
                 in_=ve[g * K_PASS:(g + 1) * K_PASS, c0:c1].rearrange("(p j) w -> p j w", j=PACK),
             )
 
+        def load_emb(m0):
+            raw = keep.tile([P, 2, PART], BF16, name="e_raw%d" % m0, align_bytes=64)
+            nc.sync.dma_start(out=raw[:], in_=emb[m0 * P:(m0 + 2) * P, :].rearrange("(m p) k -> p m k", p=P))
+            for i in range(2):
+                x_raw[m0 + i, 2] = raw[:, i, :]
+
         load_x(hidden, 0, 0, 1, 0)
         load_x(hidden, 0, 1, 1, PART)
-        load_vh(0)
         load_x(hidden, 1, 0, 2, 0)
+        load_sc(0)
+        load_vh(0)
         load_x(hidden, 2, 0, 2, 0)
-        load_ve(0, 0)
         load_x(hidden, 3, 0, 2, 0)
-        for m in range(M_TILES):
-            load_x(emb, m, 2, 1, 0)
+        load_emb(0)
+        load_emb(2)
+        load_ve(0, 0)
+        load_sc(1)
+        load_vh(1)
         load_ve(0, 1)
-        for gi in (1, 2):
-            load_vh(gi)
-            load_ve(gi, 0)
-            load_ve(gi, 1)
+        load_ve(1, 0)
+        load_ve(1, 1)
+        for n in range(2, N_TILES):
+            if n < len(SC_GROUPS):
+                load_sc(n)
+            load_vh(n)
+            load_ve(n, 0)
+            load_ve(n, 1)
 
-        turns = []
-        x_grouped, x_codes, x_scales = {}, {}, {}
-
-        def next_turn_bank():
-            b = 4 + len(turns) % 4
-            turns.append(b)
-            return bank(b)
+        x_turned, x_grouped, x_codes, x_scales = {}, {}, {}, {}
 
         def unpack_words(copy, dst, src, groups):
             copy(
@@ -121,13 +148,36 @@ def tile_multi_token_draft_logits_s1_kernel(tc, hidden, emb, vh_words, vh_scales
                 in_=src.rearrange("p (g u r) -> p g r u", g=groups, u=2),
             )
 
+        x_sorted = {}
+
+        def sort_x(m, part):
+            words = stage.tile([P, PART // 2], F32, name="x_sorted")
+            nc.vector.tensor_copy(
+                out=words[:].rearrange("p (g u r) -> p g u r", g=2, u=2),
+                in_=x_raw[m, part].bitcast(F32).rearrange("p (g r u) -> p g u r", g=2, u=2),
+            )
+            x_sorted[m, part] = words
+
+        def warm_passes(count):
+            b, spare = take_bank()
+            free_banks.append(b)
+            for i in range(count):
+                nc.tensor.matmul_mx(
+                    out=spare[:, 0:P],
+                    lhsT=zero_codes[:].bitcast(FP8X4),
+                    lhsT_scale=zero_scales[:],
+                    rhs=zero_codes[:].bitcast(FP8X4),
+                    rhs_scale=zero_scales[:],
+                    start=True,
+                    stop=True,
+                )
+
         def transpose_x(m, part):
-            words = x_raw[m, part].bitcast(F32)
-            turned = next_turn_bank()
-            for g in range(2):
-                for u in range(2):
-                    col = (2 * g + u) * P
-                    nc.tensor.transpose(turned[:, col:col + P], words[:, 256 * g + u:256 * (g + 1):2], ident[:])
+            words = x_sorted[m, part]
+            b, turned = take_bank()
+            for col in range(0, N_TILE, P):
+                nc.tensor.transpose(turned[:, col:col + P], words[:, col:col + P], ident[:])
+            free_banks.append(b)
             grouped = stage.tile([P, PART], BF16, name="x_grouped", align_bytes=64)
             unpack_words(nc.scalar.copy, grouped[:], turned[:], 2)
             x_grouped[m, part] = grouped
@@ -145,7 +195,7 @@ def tile_multi_token_draft_logits_s1_kernel(tc, hidden, emb, vh_words, vh_scales
             words = bias_cols[:].bitcast(F32)
             for n0 in range(0, N_TILES, 2):
                 tiles = min(2, N_TILES - n0)
-                turned = next_turn_bank()
+                b, turned = take_bank()
                 for i in range(tiles):
                     for u in range(2):
                         col = (2 * i + u) * P
@@ -153,10 +203,11 @@ def tile_multi_token_draft_logits_s1_kernel(tc, hidden, emb, vh_words, vh_scales
                         nc.tensor.transpose(
                             turned[:, col:col + P], words[:, word:word + 1].to_broadcast([P, P]), ident[:]
                         )
-                bias_banks.append((n0, tiles, turned))
+                bias_banks.append((n0, tiles, b, turned))
 
         def copy_bias():
-            for n0, tiles, turned in bias_banks:
+            for n0, tiles, b, turned in bias_banks:
+                free_banks.append(b)
                 unpack_words(
                     nc.vector.tensor_copy,
                     bias_rows[:, n0 * N_TILE:(n0 + tiles) * N_TILE],
@@ -167,12 +218,14 @@ def tile_multi_token_draft_logits_s1_kernel(tc, hidden, emb, vh_words, vh_scales
         ve_grouped, ve_codes, ve_scales = {}, {}, {}
 
         def interleave_ve(n, g, scalar_cols=0):
-            gi, j = place[n]
+            gi, j = place(VE_GROUPS, n)
             grouped = stage.tile([P, N_TILE, PACK], BF16, name="ve_grouped", align_bytes=64, bufs=3)
-            src = ve_raw[gi, g][:, :, j * N_TILE:(j + 1) * N_TILE].rearrange("p j w -> p w j")
-            if scalar_cols:
-                nc.scalar.copy(out=grouped[:, 0:scalar_cols, :], in_=src[:, 0:scalar_cols, :])
-            nc.vector.tensor_copy(out=grouped[:, scalar_cols:, :], in_=src[:, scalar_cols:, :])
+            src = ve_raw[gi, g][:, :, j * N_TILE:(j + 1) * N_TILE]
+            for copy, c0, c1 in ((nc.scalar.copy, 0, scalar_cols), (nc.vector.tensor_copy, scalar_cols, N_TILE)):
+                copy(
+                    out=grouped[:, c0:c1, :].rearrange("p (c i) t -> p c t i", i=4),
+                    in_=src[:, :, c0:c1].rearrange("p t (c i) -> p c t i", i=4),
+                )
             ve_grouped[n, g] = grouped
 
         def quantize_ve(n, g):
@@ -183,11 +236,12 @@ def tile_multi_token_draft_logits_s1_kernel(tc, hidden, emb, vh_words, vh_scales
             )
             ve_codes[n, g], ve_scales[n, g] = codes, scales
 
-        acc, logits = {}, {}
+        acc, acc_bank, logits = {}, {}, {}
 
         def hidden_passes(m, n):
-            gi, j = place[n]
-            acc[m, n] = bank((4 * n + m) % BANKS)
+            gi, j = place(VH_GROUPS, n)
+            si, sj = place(SC_GROUPS, n)
+            acc_bank[m, n], acc[m, n] = take_bank()
             for g in range(H_PASSES):
                 cols = slice((g % 2) * P, (g % 2 + 1) * P)
                 nc.tensor.matmul_mx(
@@ -195,13 +249,13 @@ def tile_multi_token_draft_logits_s1_kernel(tc, hidden, emb, vh_words, vh_scales
                     lhsT=x_codes[m, g // 2][:, cols].bitcast(FP8X4),
                     lhsT_scale=x_scales[m, g // 2][:, cols],
                     rhs=vh_w[gi][:, g, 2 * j * N_TILE:2 * (j + 1) * N_TILE].bitcast(FP4X4),
-                    rhs_scale=vh_s[gi][:, g, j * N_TILE:(j + 1) * N_TILE],
+                    rhs_scale=vh_s[si][:, g, sj * N_TILE:(sj + 1) * N_TILE],
                     start=(g == 0),
                     stop=False,
                 )
 
-        def emb_passes(m, n):
-            for g in range(E_PASSES):
+        def emb_passes(m, n, passes=(0, 1)):
+            for g in passes:
                 cols = slice(g * P, (g + 1) * P)
                 nc.tensor.matmul_mx(
                     out=acc[m, n][:],
@@ -213,61 +267,125 @@ def tile_multi_token_draft_logits_s1_kernel(tc, hidden, emb, vh_words, vh_scales
                     stop=(g == E_PASSES - 1),
                 )
 
-        def add_bias(m, n):
-            z = keep.tile([P, N_TILE], F32, name="logits%d_%d" % (m, n))
+        def add_bias(m, n, c0=0, c1=N_TILE):
+            if c0 == 0:
+                logits[m, n] = keep.tile([P, N_TILE], F32, name="logits%d_%d" % (m, n))
+                free_banks.append(acc_bank[m, n])
+            z = logits[m, n][:, c0:c1]
             nc.vector.tensor_tensor(
-                out=z[:], in0=acc[m, n][:], in1=bias_rows[:, n * N_TILE:(n + 1) * N_TILE], op=ALU.add
+                out=z, in0=acc[m, n][:, c0:c1], in1=bias_rows[:, n * N_TILE + c0:n * N_TILE + c1], op=ALU.add
             )
-            nc.scalar.activation(out=z[:], in_=z[:], func=ACT.Tanh, scale=1.0 / CAP)
-            logits[m, n] = z
+            nc.scalar.activation(out=z, in_=z, func=ACT.Tanh, scale=1.0 / CAP)
 
-        def finish(m, n, on_vector):
-            z = logits[m, n]
-            if on_vector:
-                nc.vector.tensor_scalar(out=z[:], in0=z[:], scalar1=CAP, scalar2=None, op0=ALU.mult)
-            else:
-                nc.scalar.activation(out=z[:], in_=z[:], func=ACT.Copy, scale=CAP)
-            nc.sync.dma_start(out=out[m * P:(m + 1) * P, n * N_TILE:(n + 1) * N_TILE], in_=z[:])
+        def finish(m, n, c0=0, c1=N_TILE):
+            z = logits[m, n][:, c0:c1]
+            nc.vector.tensor_scalar(out=z, in0=z, scalar1=CAP, scalar2=None, op0=ALU.mult)
+            nc.sync.dma_start(out=out[m * P:(m + 1) * P, n * N_TILE + c0:n * N_TILE + c1], in_=z)
 
-        transpose_x(0, 0)
-        transpose_x(0, 1)
+        def split_ve(n, g):
+            interleave_ve(n, g, scalar_cols=SCALAR_COLS)
+
+        warm_passes(WARM_PASSES)
+        for part in range(2):
+            sort_x(0, part)
+            transpose_x(0, part)
         transpose_bias()
+        for part in range(2):
+            sort_x(1, part)
+            transpose_x(1, part)
         quantize_x(0, 0)
         quantize_x(0, 1)
         copy_bias()
+        warm_passes(4)
         hidden_passes(0, 0)
-        for m in (1, 2):
-            for part in (0, 1):
-                transpose_x(m, part)
-                quantize_x(m, part)
+        quantize_x(1, 0)
+        sort_x(2, 0)
+        sort_x(2, 1)
+        quantize_x(1, 1)
+        transpose_x(2, 0)
+        transpose_x(2, 1)
         hidden_passes(1, 0)
-        interleave_ve(0, 0)
-        for part in (0, 1):
-            transpose_x(3, part)
-            quantize_x(3, part)
+        sort_x(3, 0)
+        sort_x(3, 1)
+        transpose_x(3, 0)
+        transpose_x(3, 1)
+        quantize_x(2, 0)
+        quantize_x(2, 1)
+        sort_x(0, 2)
+        sort_x(1, 2)
         hidden_passes(2, 0)
-        quantize_ve(0, 0)
-        for m in range(M_TILES):
-            transpose_x(m, 2)
-            quantize_x(m, 2)
-            if m == 1:
-                interleave_ve(0, 1)
-        quantize_ve(0, 1)
+        transpose_x(0, 2)
+        transpose_x(1, 2)
+        quantize_x(3, 0)
+        quantize_x(3, 1)
+        sort_x(2, 2)
+        sort_x(3, 2)
+        transpose_x(2, 2)
+        transpose_x(3, 2)
         hidden_passes(3, 0)
+        interleave_ve(0, 0, scalar_cols=64)
+        quantize_x(0, 2)
+        quantize_x(1, 2)
+        quantize_ve(0, 0)
+        quantize_x(2, 2)
+        quantize_x(3, 2)
+        hidden_passes(0, 1)
+        hidden_passes(1, 1)
+        interleave_ve(0, 1, scalar_cols=192)
+        for m in range(M_TILES):
+            emb_passes(m, 0, (0,))
+        interleave_ve(1, 0, scalar_cols=192)
+        quantize_ve(0, 1)
+        hidden_passes(2, 1)
+        for m in range(M_TILES):
+            emb_passes(m, 0, (1,))
+        split_ve(1, 1)
+        quantize_ve(1, 0)
+        hidden_passes(3, 1)
+        add_bias(0, 0)
+        quantize_ve(1, 1)
+        for m in range(M_TILES):
+            emb_passes(m, 1)
+        for m in range(1, M_TILES):
+            add_bias(m, 0)
+            finish(m - 1, 0)
 
-        for n in range(N_TILES):
-            more = n + 1 < N_TILES
-            for m in range(M_TILES):
-                if n > 0:
+        for n in range(2, N_TILES):
+            split_ve(n, 0)
+            finish(3, n - 2)
+            split_ve(n, 1)
+            add_bias(0, n - 1)
+            quantize_ve(n, 0)
+            add_bias(1, n - 1)
+            add_bias(2, n - 1)
+            quantize_ve(n, 1)
+            add_bias(3, n - 1)
+            for m in range(3):
+                finish(m, n - 1)
+            if n < N_TILES - 1:
+                for m in range(M_TILES):
                     hidden_passes(m, n)
-                emb_passes(m, n)
-                if more and m < 2:
-                    interleave_ve(n + 1, m, scalar_cols=128)
-                add_bias(m, n)
-                if more and m in (1, 2):
-                    quantize_ve(n + 1, m - 1)
-                if more:
-                    finish(m, n, False)
-                elif m > 0:
-                    finish(m - 1, n, True)
-        finish(M_TILES - 1, N_TILES - 1, True)
+                for m in range(M_TILES):
+                    emb_passes(m, n)
+        n = N_TILES - 1
+        hidden_passes(0, n)
+        hidden_passes(1, n)
+        emb_passes(0, n)
+        emb_passes(1, n)
+        add_bias(0, n)
+        finish(3, n - 1)
+        add_bias(1, n)
+        hidden_passes(2, n)
+        emb_passes(2, n)
+        finish(0, n)
+        finish(1, n)
+        add_bias(2, n)
+        m = M_TILES - 1
+        hidden_passes(m, n)
+        emb_passes(m, n)
+        half = N_TILE // 2
+        finish(m - 1, n)
+        add_bias(m, n, 0, half)
+        add_bias(m, n, half, N_TILE)
+        finish(m, n, 0, half)
+        finish(m, n, half, N_TILE)

@@ -29,8 +29,8 @@ PART = 2 * K_PASS
 VH_GROUPS = ((0,), (1,), (2,), (3,), (4,))
 VE_GROUPS = ((0,), (1,), (2,), (3,), (4,))
 SC_GROUPS = ((0,), (1,), (2,), (3, 4))
-WARM_PASSES = 8
-SCALAR_COLS = 352
+WARM_PASSES = 13
+SCALAR_COLS = 320
 BANKS = 8
 
 
@@ -64,7 +64,6 @@ def tile_multi_token_draft_logits_s1_kernel(tc, hidden, emb, vh_words, vh_scales
             return [(gi, group.index(n)) for gi, group in enumerate(groups) if n in group][0]
 
         ident = keep.tile([P, P], F32, name="ident")
-        make_identity(nc, ident[:])
         bias_cols = keep.tile([P, N_TILES * 16], BF16, name="bias_cols")
         nc.scalar.dma_start(
             out=bias_cols[:].rearrange("p (n c) -> p n c", c=16)[:, :, 0:PACK],
@@ -74,12 +73,12 @@ def tile_multi_token_draft_logits_s1_kernel(tc, hidden, emb, vh_words, vh_scales
         zero_codes = keep.tile([P, P], U32, name="zero_codes", align_bytes=64)
         zero_scales = keep.tile([P, P], U8, name="zero_scales", align_bytes=64)
         warm = keep.tile([P, 1], F32, name="warm")
-        nc.vector.memset(zeros[:], 0.0)
+        nc.vector.memset(zeros[:].bitcast(I32), 0)
         nc.vector.memset(vh_s[0][:].rearrange("p g n -> p (g n)").bitcast(I32), 0)
         nc.vector.quantize_mx(out=zero_codes[:].bitcast(FP8X4), scales=zero_scales[:], in_=zeros[:])
         nc.scalar.activation(out=warm[:], in_=zeros[:, 0:1], func=ACT.Tanh)
-        for gi in range(1, len(SC_GROUPS)):
-            nc.vector.memset(vh_s[gi][:].rearrange("p g n -> p (g n)").bitcast(I32), 0)
+        nc.vector.memset(ident[:], 0.0)
+        make_identity(nc, ident[:], nomemset=True)
 
         def load_x(src, m, first_part, parts, col0):
             raw = keep.tile([P, parts * PART], BF16, name="x_raw%d_%d" % (m, first_part), align_bytes=64)
@@ -123,22 +122,11 @@ def tile_multi_token_draft_logits_s1_kernel(tc, hidden, emb, vh_words, vh_scales
         load_x(hidden, 1, 0, 2, 0)
         load_sc(0)
         load_vh(0)
-        load_x(hidden, 2, 0, 2, 0)
+        load_x(hidden, 2, 0, 1, 0)
+        load_x(hidden, 2, 1, 1, PART)
         load_x(hidden, 3, 0, 2, 0)
         load_emb(0)
         load_emb(2)
-        load_ve(0, 0)
-        load_sc(1)
-        load_vh(1)
-        load_ve(0, 1)
-        load_ve(1, 0)
-        load_ve(1, 1)
-        for n in range(2, N_TILES):
-            if n < len(SC_GROUPS):
-                load_sc(n)
-            load_vh(n)
-            load_ve(n, 0)
-            load_ve(n, 1)
 
         x_turned, x_grouped, x_codes, x_scales = {}, {}, {}, {}
 
@@ -209,7 +197,7 @@ def tile_multi_token_draft_logits_s1_kernel(tc, hidden, emb, vh_words, vh_scales
             for n0, tiles, b, turned in bias_banks:
                 free_banks.append(b)
                 unpack_words(
-                    nc.vector.tensor_copy,
+                    nc.scalar.copy,
                     bias_rows[:, n0 * N_TILE:(n0 + tiles) * N_TILE],
                     turned[:, 0:tiles * 2 * P],
                     tiles,
@@ -222,6 +210,8 @@ def tile_multi_token_draft_logits_s1_kernel(tc, hidden, emb, vh_words, vh_scales
             grouped = stage.tile([P, N_TILE, PACK], BF16, name="ve_grouped", align_bytes=64, bufs=3)
             src = ve_raw[gi, g][:, :, j * N_TILE:(j + 1) * N_TILE]
             for copy, c0, c1 in ((nc.scalar.copy, 0, scalar_cols), (nc.vector.tensor_copy, scalar_cols, N_TILE)):
+                if c0 == c1:
+                    continue
                 copy(
                     out=grouped[:, c0:c1, :].rearrange("p (c i) t -> p c t i", i=4),
                     in_=src[:, :, c0:c1].rearrange("p t (c i) -> p c t i", i=4),
@@ -267,20 +257,36 @@ def tile_multi_token_draft_logits_s1_kernel(tc, hidden, emb, vh_words, vh_scales
                     stop=(g == E_PASSES - 1),
                 )
 
+        for n in range(N_TILES):
+            logits[n] = keep.tile([P, M_TILES, N_TILE], F32, name="logits%d" % n)
+
         def add_bias(m, n, c0=0, c1=N_TILE):
             if c0 == 0:
-                logits[m, n] = keep.tile([P, N_TILE], F32, name="logits%d_%d" % (m, n))
                 free_banks.append(acc_bank[m, n])
-            z = logits[m, n][:, c0:c1]
             nc.vector.tensor_tensor(
-                out=z, in0=acc[m, n][:, c0:c1], in1=bias_rows[:, n * N_TILE + c0:n * N_TILE + c1], op=ALU.add
+                out=logits[n][:, m, c0:c1],
+                in0=acc[m, n][:, c0:c1],
+                in1=bias_rows[:, n * N_TILE + c0:n * N_TILE + c1],
+                op=ALU.add,
             )
+
+        def squash(m, n, c0=0, c1=N_TILE):
+            z = logits[n][:, m, c0:c1]
             nc.scalar.activation(out=z, in_=z, func=ACT.Tanh, scale=1.0 / CAP)
 
-        def finish(m, n, c0=0, c1=N_TILE):
-            z = logits[m, n][:, c0:c1]
-            nc.vector.tensor_scalar(out=z, in0=z, scalar1=CAP, scalar2=None, op0=ALU.mult)
-            nc.sync.dma_start(out=out[m * P:(m + 1) * P, n * N_TILE + c0:n * N_TILE + c1], in_=z)
+        def store(m0, m1, n, c0=0, c1=N_TILE):
+            nc.sync.dma_start(
+                out=out[m0 * P:m1 * P, n * N_TILE + c0:n * N_TILE + c1].rearrange("(m p) c -> p m c", p=P),
+                in_=logits[n][:, m0:m1, c0:c1],
+            )
+
+        def finish(m0, m1, n, c0=0, c1=N_TILE, on_scalar=False):
+            z = logits[n][:, m0:m1, c0:c1]
+            if on_scalar:
+                nc.scalar.activation(out=z, in_=z, func=ACT.Copy, scale=CAP)
+            else:
+                nc.vector.tensor_scalar(out=z, in0=z, scalar1=CAP, scalar2=None, op0=ALU.mult)
+            store(m0, m1, n, c0, c1)
 
         def split_ve(n, g):
             interleave_ve(n, g, scalar_cols=SCALAR_COLS)
@@ -289,6 +295,21 @@ def tile_multi_token_draft_logits_s1_kernel(tc, hidden, emb, vh_words, vh_scales
         for part in range(2):
             sort_x(0, part)
             transpose_x(0, part)
+        for gi in range(1, len(SC_GROUPS)):
+            nc.vector.memset(vh_s[gi][:].rearrange("p g n -> p (g n)").bitcast(I32), 0)
+        load_sc(1)
+        load_vh(1)
+        load_ve(0, 0)
+        load_ve(0, 1)
+        load_ve(1, 0)
+        load_ve(1, 1)
+        for n in range(2, N_TILES):
+            load_ve(n, 0)
+            load_ve(n, 1)
+            if n < len(SC_GROUPS):
+                load_sc(n)
+            load_vh(n)
+
         transpose_bias()
         for part in range(2):
             sort_x(1, part)
@@ -298,94 +319,84 @@ def tile_multi_token_draft_logits_s1_kernel(tc, hidden, emb, vh_words, vh_scales
         copy_bias()
         warm_passes(4)
         hidden_passes(0, 0)
-        quantize_x(1, 0)
-        sort_x(2, 0)
-        sort_x(2, 1)
-        quantize_x(1, 1)
-        transpose_x(2, 0)
-        transpose_x(2, 1)
+        for part in range(2):
+            sort_x(2, part)
+            quantize_x(1, part)
+            transpose_x(2, part)
         hidden_passes(1, 0)
-        sort_x(3, 0)
-        sort_x(3, 1)
-        transpose_x(3, 0)
-        transpose_x(3, 1)
+        for part in range(2):
+            sort_x(3, part)
+            transpose_x(3, part)
         quantize_x(2, 0)
         quantize_x(2, 1)
-        sort_x(0, 2)
-        sort_x(1, 2)
         hidden_passes(2, 0)
-        transpose_x(0, 2)
-        transpose_x(1, 2)
+        for m in (0, 1):
+            sort_x(m, 2)
+            transpose_x(m, 2)
         quantize_x(3, 0)
         quantize_x(3, 1)
-        sort_x(2, 2)
-        sort_x(3, 2)
-        transpose_x(2, 2)
-        transpose_x(3, 2)
         hidden_passes(3, 0)
-        interleave_ve(0, 0, scalar_cols=64)
+        for m in (2, 3):
+            sort_x(m, 2)
+            transpose_x(m, 2)
         quantize_x(0, 2)
         quantize_x(1, 2)
-        quantize_ve(0, 0)
+        interleave_ve(0, 0, scalar_cols=0)
         quantize_x(2, 2)
+        quantize_ve(0, 0)
         quantize_x(3, 2)
-        hidden_passes(0, 1)
-        hidden_passes(1, 1)
+        for m in range(M_TILES):
+            hidden_passes(m, 1)
         interleave_ve(0, 1, scalar_cols=192)
-        for m in range(M_TILES):
-            emb_passes(m, 0, (0,))
-        interleave_ve(1, 0, scalar_cols=192)
+        interleave_ve(1, 0, scalar_cols=256)
         quantize_ve(0, 1)
-        hidden_passes(2, 1)
-        for m in range(M_TILES):
-            emb_passes(m, 0, (1,))
         split_ve(1, 1)
         quantize_ve(1, 0)
-        hidden_passes(3, 1)
-        add_bias(0, 0)
         quantize_ve(1, 1)
+        for g in range(E_PASSES):
+            for m in range(M_TILES):
+                emb_passes(m, 0, (g,))
         for m in range(M_TILES):
             emb_passes(m, 1)
-        for m in range(1, M_TILES):
-            add_bias(m, 0)
-            finish(m - 1, 0)
-
-        for n in range(2, N_TILES):
-            split_ve(n, 0)
-            finish(3, n - 2)
-            split_ve(n, 1)
-            add_bias(0, n - 1)
-            quantize_ve(n, 0)
-            add_bias(1, n - 1)
-            add_bias(2, n - 1)
-            quantize_ve(n, 1)
-            add_bias(3, n - 1)
-            for m in range(3):
-                finish(m, n - 1)
-            if n < N_TILES - 1:
+        for n in range(3):
+            for m in range(M_TILES):
+                add_bias(m, n)
+            split_ve(n + 2, 0)
+            split_ve(n + 2, 1)
+            for m in range(M_TILES):
+                squash(m, n)
+            quantize_ve(n + 2, 0)
+            quantize_ve(n + 2, 1)
+            if n < 2:
+                finish(0, 2, n)
+                finish(2, 4, n)
+            if n < 2:
                 for m in range(M_TILES):
-                    hidden_passes(m, n)
+                    hidden_passes(m, n + 2)
                 for m in range(M_TILES):
-                    emb_passes(m, n)
+                    emb_passes(m, n + 2)
+        finish(0, 2, 2)
+        finish(2, 4, 2, on_scalar=True)
+        for m in range(M_TILES):
+            add_bias(m, 3)
+            squash(m, 3)
         n = N_TILES - 1
-        hidden_passes(0, n)
-        hidden_passes(1, n)
-        emb_passes(0, n)
-        emb_passes(1, n)
+        for m in range(M_TILES):
+            hidden_passes(m, n)
+            emb_passes(m, n)
+        finish(0, 2, 3)
         add_bias(0, n)
-        finish(3, n - 1)
-        add_bias(1, n)
-        hidden_passes(2, n)
-        emb_passes(2, n)
-        finish(0, n)
-        finish(1, n)
-        add_bias(2, n)
+        finish(2, 4, 3)
+        squash(0, n)
+        for m in (1, 2):
+            add_bias(m, n)
+            squash(m, n)
+            finish(m - 1, m, n)
+        finish(2, 3, n, on_scalar=True)
         m = M_TILES - 1
-        hidden_passes(m, n)
-        emb_passes(m, n)
         half = N_TILE // 2
-        finish(m - 1, n)
-        add_bias(m, n, 0, half)
-        add_bias(m, n, half, N_TILE)
-        finish(m, n, 0, half)
-        finish(m, n, half, N_TILE)
+        for c0 in (0, half):
+            add_bias(m, n, c0, c0 + half)
+            squash(m, n, c0, c0 + half)
+        for c0 in (0, half):
+            finish(m, m + 1, n, c0, c0 + half)

@@ -97,11 +97,11 @@ def tile_multi_token_draft_logits_s1_kernel(tc, hidden, emb, vh_words, vh_scales
                     in_=vh_scales[:, r:16:4, c0:c1].rearrange("g q n -> q g n").bitcast(I32),
                 )
 
-        def load_vh(gi):
+        def load_vh(gi, g0=0, g1=H_PASSES):
             c0, c1 = group_cols(VH_GROUPS[gi])
             nc.sync.dma_start(
-                out=vh_w[gi][:].bitcast(I32),
-                in_=vh_words[:, :, 2 * c0:2 * c1].rearrange("g p b -> p g b").bitcast(I32),
+                out=vh_w[gi][:, g0:g1, :].bitcast(I32),
+                in_=vh_words[g0:g1, :, 2 * c0:2 * c1].rearrange("g p b -> p g b").bitcast(I32),
             )
 
         def load_ve(gi, g):
@@ -121,7 +121,8 @@ def tile_multi_token_draft_logits_s1_kernel(tc, hidden, emb, vh_words, vh_scales
         load_x(hidden, 0, 1, 1, PART)
         load_x(hidden, 1, 0, 2, 0)
         load_sc(0)
-        load_vh(0)
+        load_vh(0, 0, 2)
+        load_vh(0, 2, 4)
         load_x(hidden, 2, 0, 1, 0)
         load_x(hidden, 2, 1, 1, PART)
         load_x(hidden, 3, 0, 2, 0)
@@ -228,11 +229,12 @@ def tile_multi_token_draft_logits_s1_kernel(tc, hidden, emb, vh_words, vh_scales
 
         acc, acc_bank, logits = {}, {}, {}
 
-        def hidden_passes(m, n):
+        def hidden_passes(m, n, g0=0, g1=H_PASSES):
             gi, j = place(VH_GROUPS, n)
             si, sj = place(SC_GROUPS, n)
-            acc_bank[m, n], acc[m, n] = take_bank()
-            for g in range(H_PASSES):
+            if g0 == 0:
+                acc_bank[m, n], acc[m, n] = take_bank()
+            for g in range(g0, g1):
                 cols = slice((g % 2) * P, (g % 2 + 1) * P)
                 nc.tensor.matmul_mx(
                     out=acc[m, n][:],
@@ -317,28 +319,31 @@ def tile_multi_token_draft_logits_s1_kernel(tc, hidden, emb, vh_words, vh_scales
         quantize_x(0, 0)
         quantize_x(0, 1)
         copy_bias()
-        warm_passes(4)
         hidden_passes(0, 0)
-        for part in range(2):
-            sort_x(2, part)
-            quantize_x(1, part)
-            transpose_x(2, part)
-        hidden_passes(1, 0)
+        quantize_x(1, 0)
+        sort_x(2, 0)
+        quantize_x(1, 1)
+        sort_x(2, 1)
+        hidden_passes(1, 0, 0, 2)
+        transpose_x(2, 0)
+        transpose_x(2, 1)
+        hidden_passes(1, 0, 2, 4)
         for part in range(2):
             sort_x(3, part)
             transpose_x(3, part)
         quantize_x(2, 0)
         quantize_x(2, 1)
         hidden_passes(2, 0)
-        for m in (0, 1):
-            sort_x(m, 2)
-            transpose_x(m, 2)
+        sort_x(0, 2)
+        sort_x(1, 2)
         quantize_x(3, 0)
-        quantize_x(3, 1)
-        hidden_passes(3, 0)
+        transpose_x(0, 2)
+        transpose_x(1, 2)
         for m in (2, 3):
             sort_x(m, 2)
             transpose_x(m, 2)
+        quantize_x(3, 1)
+        hidden_passes(3, 0)
         quantize_x(0, 2)
         quantize_x(1, 2)
         interleave_ve(0, 0, scalar_cols=0)
@@ -375,7 +380,7 @@ def tile_multi_token_draft_logits_s1_kernel(tc, hidden, emb, vh_words, vh_scales
                     hidden_passes(m, n + 2)
                 for m in range(M_TILES):
                     emb_passes(m, n + 2)
-        finish(0, 2, 2)
+        finish(0, 2, 2, on_scalar=True)
         finish(2, 4, 2, on_scalar=True)
         for m in range(M_TILES):
             add_bias(m, 3)

from contextlib import ExitStack

import concourse.mybir as mybir
from concourse.masks import make_identity

T, D, E, V = 512, 2048, 1024, 2560
CAP = 4.0
FLOPS = 2 * T * (D + E) * V

F32 = mybir.dt.float32
BF16 = mybir.dt.bfloat16
I32 = mybir.dt.int32
U32 = mybir.dt.uint32
U8 = mybir.dt.uint8
FP8X4 = mybir.dt.float8_e4m3fn_x4
FP4X4 = mybir.dt.float4_e2m1fn_x4
ALU = mybir.AluOpType
ACT = mybir.ActivationFunctionType

P = 128
PACK = 4
K_PASS = P * PACK
N_TILE = 512
M_TILES = T // P
N_TILES = V // N_TILE
H_PASSES = D // K_PASS
E_PASSES = E // K_PASS
PART = 2 * K_PASS
VH_GROUPS = ((0,), (1,), (2,), (3,), (4,))
VE_GROUPS = ((0,), (1,), (2,), (3,), (4,))
SC_GROUPS = ((0,), (1,), (2,), (3, 4))
WARM_PASSES = 13
SCALAR_COLS = 320
BANKS = 8


def tile_multi_token_draft_logits_s1_kernel(tc, hidden, emb, vh_words, vh_scales, ve, bias, out):
    nc = tc.nc
    with ExitStack() as ctx:
        keep = ctx.enter_context(tc.tile_pool(name="keep", bufs=1))
        stage = ctx.enter_context(tc.tile_pool(name="stage", bufs=4))
        psum = ctx.enter_context(tc.psum_pool(name="psum", bufs=1))
        ctx.enter_context(tc.manual_schedule())

        free_banks = list(range(BANKS))

        def take_bank():
            b = free_banks.pop(0)
            return b, psum.tile([P, N_TILE], F32, name="bank%d" % b, tag="bank%d" % b)

        x_raw = {}
        vh_w, vh_s, ve_raw = {}, {}, {}
        for gi, group in enumerate(VH_GROUPS):
            vh_w[gi] = keep.tile([P, H_PASSES, 2 * N_TILE * len(group)], U8, name="vh_w%d" % gi, align_bytes=64)
        for gi, group in enumerate(SC_GROUPS):
            vh_s[gi] = keep.tile([P, H_PASSES, N_TILE * len(group)], U8, name="vh_s%d" % gi, align_bytes=64)
        for gi, group in enumerate(VE_GROUPS):
            for g in range(E_PASSES):
                ve_raw[gi, g] = keep.tile(
                    [P, PACK, N_TILE * len(group)], BF16, name="ve_raw%d_%d" % (gi, g), align_bytes=64
                )

        def place(groups, n):
            return [(gi, group.index(n)) for gi, group in enumerate(groups) if n in group][0]

        ident = keep.tile([P, P], F32, name="ident")
        bias_cols = keep.tile([P, N_TILES * 16], BF16, name="bias_cols")
        nc.scalar.dma_start(
            out=bias_cols[:].rearrange("p (n c) -> p n c", c=16)[:, :, 0:PACK],
            in_=bias.rearrange("(n p t) -> p n t", p=P, t=PACK),
        )
        zeros = keep.tile([P, K_PASS], BF16, name="zeros", align_bytes=64)
        zero_codes = keep.tile([P, P], U32, name="zero_codes", align_bytes=64)
        zero_scales = keep.tile([P, P], U8, name="zero_scales", align_bytes=64)
        warm = keep.tile([P, 1], F32, name="warm")
        nc.vector.memset(zeros[:].bitcast(I32), 0)
        nc.vector.memset(vh_s[0][:].rearrange("p g n -> p (g n)").bitcast(I32), 0)
        nc.vector.quantize_mx(out=zero_codes[:].bitcast(FP8X4), scales=zero_scales[:], in_=zeros[:])
        nc.scalar.activation(out=warm[:], in_=zeros[:, 0:1], func=ACT.Tanh)
        nc.vector.memset(ident[:], 0.0)
        make_identity(nc, ident[:], nomemset=True)

        def load_x(src, m, first_part, parts, col0):
            raw = keep.tile([P, parts * PART], BF16, name="x_raw%d_%d" % (m, first_part), align_bytes=64)
            nc.sync.dma_start(out=raw[:], in_=src[m * P:(m + 1) * P, col0:col0 + parts * PART])
            for i in range(parts):
                x_raw[m, first_part + i] = raw[:, i * PART:(i + 1) * PART]

        def group_cols(group):
            return group[0] * N_TILE, (group[-1] + 1) * N_TILE

        def load_sc(gi):
            c0, c1 = group_cols(SC_GROUPS[gi])
            for r in range(4):
                nc.sync.dma_start(
                    out=vh_s[gi][r:P:32, :, :].bitcast(I32),
                    in_=vh_scales[:, r:16:4, c0:c1].rearrange("g q n -> q g n").bitcast(I32),
                )

        def load_vh(gi, g0=0, g1=H_PASSES):
            c0, c1 = group_cols(VH_GROUPS[gi])
            nc.sync.dma_start(
                out=vh_w[gi][:, g0:g1, :].bitcast(I32),
                in_=vh_words[g0:g1, :, 2 * c0:2 * c1].rearrange("g p b -> p g b").bitcast(I32),
            )

        def load_ve(gi, g):
            c0, c1 = group_cols(VE_GROUPS[gi])
            nc.sync.dma_start(
                out=ve_raw[gi, g][:],
                in_=ve[g * K_PASS:(g + 1) * K_PASS, c0:c1].rearrange("(p j) w -> p j w", j=PACK),
            )

        def load_emb(m0):
            raw = keep.tile([P, 2, PART], BF16, name="e_raw%d" % m0, align_bytes=64)
            nc.sync.dma_start(out=raw[:], in_=emb[m0 * P:(m0 + 2) * P, :].rearrange("(m p) k -> p m k", p=P))
            for i in range(2):
                x_raw[m0 + i, 2] = raw[:, i, :]

        load_x(hidden, 0, 0, 1, 0)
        load_x(hidden, 0, 1, 1, PART)
        load_x(hidden, 1, 0, 2, 0)
        load_sc(0)
        load_vh(0, 0, 2)
        load_vh(0, 2, 4)
        load_x(hidden, 2, 0, 1, 0)
        load_x(hidden, 2, 1, 1, PART)
        load_x(hidden, 3, 0, 2, 0)
        load_emb(0)
        load_emb(2)

        x_turned, x_grouped, x_codes, x_scales = {}, {}, {}, {}

        def unpack_words(copy, dst, src, groups):
            copy(
                out=dst.bitcast(F32).rearrange("p (g r u) -> p g r u", g=groups, u=2),
                in_=src.rearrange("p (g u r) -> p g r u", g=groups, u=2),
            )

        x_sorted = {}

        def sort_x(m, part):
            words = stage.tile([P, PART // 2], F32, name="x_sorted")
            nc.vector.tensor_copy(
                out=words[:].rearrange("p (g u r) -> p g u r", g=2, u=2),
                in_=x_raw[m, part].bitcast(F32).rearrange("p (g r u) -> p g u r", g=2, u=2),
            )
            x_sorted[m, part] = words

        def warm_passes(count):
            b, spare = take_bank()
            free_banks.append(b)
            for i in range(count):
                nc.tensor.matmul_mx(
                    out=spare[:, 0:P],
                    lhsT=zero_codes[:].bitcast(FP8X4),
                    lhsT_scale=zero_scales[:],
                    rhs=zero_codes[:].bitcast(FP8X4),
                    rhs_scale=zero_scales[:],
                    start=True,
                    stop=True,
                )

        def transpose_x(m, part):
            words = x_sorted[m, part]
            b, turned = take_bank()
            for col in range(0, N_TILE, P):
                nc.tensor.transpose(turned[:, col:col + P], words[:, col:col + P], ident[:])
            free_banks.append(b)
            grouped = stage.tile([P, PART], BF16, name="x_grouped", align_bytes=64)
            unpack_words(nc.scalar.copy, grouped[:], turned[:], 2)
            x_grouped[m, part] = grouped

        def quantize_x(m, part):
            codes = keep.tile([P, 2 * P], U32, name="x_codes%d_%d" % (m, part), align_bytes=64)
            scales = keep.tile([P, 2 * P], U8, name="x_scales%d_%d" % (m, part), align_bytes=64)
            nc.vector.quantize_mx(out=codes[:].bitcast(FP8X4), scales=scales[:], in_=x_grouped[m, part][:])
            x_codes[m, part], x_scales[m, part] = codes, scales

        bias_rows = keep.tile([P, V], BF16, name="bias_rows")
        bias_banks = []

        def transpose_bias():
            words = bias_cols[:].bitcast(F32)
            for n0 in range(0, N_TILES, 2):
                tiles = min(2, N_TILES - n0)
                b, turned = take_bank()
                for i in range(tiles):
                    for u in range(2):
                        col = (2 * i + u) * P
                        word = (n0 + i) * 8 + u
                        nc.tensor.transpose(
                            turned[:, col:col + P], words[:, word:word + 1].to_broadcast([P, P]), ident[:]
                        )
                bias_banks.append((n0, tiles, b, turned))

        def copy_bias():
            for n0, tiles, b, turned in bias_banks:
                free_banks.append(b)
                unpack_words(
                    nc.scalar.copy,
                    bias_rows[:, n0 * N_TILE:(n0 + tiles) * N_TILE],
                    turned[:, 0:tiles * 2 * P],
                    tiles,
                )

        ve_grouped, ve_codes, ve_scales = {}, {}, {}

        def interleave_ve(n, g, scalar_cols=0):
            gi, j = place(VE_GROUPS, n)
            grouped = stage.tile([P, N_TILE, PACK], BF16, name="ve_grouped", align_bytes=64, bufs=3)
            src = ve_raw[gi, g][:, :, j * N_TILE:(j + 1) * N_TILE]
            for copy, c0, c1 in ((nc.scalar.copy, 0, scalar_cols), (nc.vector.tensor_copy, scalar_cols, N_TILE)):
                if c0 == c1:
                    continue
                copy(
                    out=grouped[:, c0:c1, :].rearrange("p (c i) t -> p c t i", i=4),
                    in_=src[:, :, c0:c1].rearrange("p t (c i) -> p c t i", i=4),
                )
            ve_grouped[n, g] = grouped

        def quantize_ve(n, g):
            codes = keep.tile([P, N_TILE], U32, name="ve_codes%d_%d" % (n, g), align_bytes=64)
            scales = keep.tile([P, N_TILE], U8, name="ve_scales%d_%d" % (n, g), align_bytes=64)
            nc.vector.quantize_mx(
                out=codes[:].bitcast(FP8X4), scales=scales[:], in_=ve_grouped[n, g][:].rearrange("p w j -> p (w j)")
            )
            ve_codes[n, g], ve_scales[n, g] = codes, scales

        acc, acc_bank, logits = {}, {}, {}

        def hidden_passes(m, n, g0=0, g1=H_PASSES):
            gi, j = place(VH_GROUPS, n)
            si, sj = place(SC_GROUPS, n)
            if g0 == 0:
                acc_bank[m, n], acc[m, n] = take_bank()
            for g in range(g0, g1):
                cols = slice((g % 2) * P, (g % 2 + 1) * P)
                nc.tensor.matmul_mx(
                    out=acc[m, n][:],
                    lhsT=x_codes[m, g // 2][:, cols].bitcast(FP8X4),
                    lhsT_scale=x_scales[m, g // 2][:, cols],
                    rhs=vh_w[gi][:, g, 2 * j * N_TILE:2 * (j + 1) * N_TILE].bitcast(FP4X4),
                    rhs_scale=vh_s[si][:, g, sj * N_TILE:(sj + 1) * N_TILE],
                    start=(g == 0),
                    stop=False,
                )

        def emb_passes(m, n, passes=(0, 1)):
            for g in passes:
                cols = slice(g * P, (g + 1) * P)
                nc.tensor.matmul_mx(
                    out=acc[m, n][:],
                    lhsT=x_codes[m, 2][:, cols].bitcast(FP8X4),
                    lhsT_scale=x_scales[m, 2][:, cols],
                    rhs=ve_codes[n, g][:].bitcast(FP8X4),
                    rhs_scale=ve_scales[n, g][:],
                    start=False,
                    stop=(g == E_PASSES - 1),
                )

        for n in range(N_TILES):
            logits[n] = keep.tile([P, M_TILES, N_TILE], F32, name="logits%d" % n)

        def add_bias(m, n, c0=0, c1=N_TILE):
            if c0 == 0:
                free_banks.append(acc_bank[m, n])
            nc.vector.tensor_tensor(
                out=logits[n][:, m, c0:c1],
                in0=acc[m, n][:, c0:c1],
                in1=bias_rows[:, n * N_TILE + c0:n * N_TILE + c1],
                op=ALU.add,
            )

        def squash(m, n, c0=0, c1=N_TILE):
            z = logits[n][:, m, c0:c1]
            nc.scalar.activation(out=z, in_=z, func=ACT.Tanh, scale=1.0 / CAP)

        def store(m0, m1, n, c0=0, c1=N_TILE):
            nc.sync.dma_start(
                out=out[m0 * P:m1 * P, n * N_TILE + c0:n * N_TILE + c1].rearrange("(m p) c -> p m c", p=P),
                in_=logits[n][:, m0:m1, c0:c1],
            )

        def finish(m0, m1, n, c0=0, c1=N_TILE, on_scalar=False):
            z = logits[n][:, m0:m1, c0:c1]
            if on_scalar:
                nc.scalar.activation(out=z, in_=z, func=ACT.Copy, scale=CAP)
            else:
                nc.vector.tensor_scalar(out=z, in0=z, scalar1=CAP, scalar2=None, op0=ALU.mult)
            store(m0, m1, n, c0, c1)

        def split_ve(n, g):
            interleave_ve(n, g, scalar_cols=SCALAR_COLS)

        warm_passes(WARM_PASSES)
        for part in range(2):
            sort_x(0, part)
            transpose_x(0, part)
        for gi in range(1, len(SC_GROUPS)):
            nc.vector.memset(vh_s[gi][:].rearrange("p g n -> p (g n)").bitcast(I32), 0)
        load_sc(1)
        load_vh(1)
        load_ve(0, 0)
        load_ve(0, 1)
        load_ve(1, 0)
        load_ve(1, 1)
        for n in range(2, N_TILES):
            load_ve(n, 0)
            load_ve(n, 1)
            if n < len(SC_GROUPS):
                load_sc(n)
            load_vh(n)

        transpose_bias()
        for part in range(2):
            sort_x(1, part)
            transpose_x(1, part)
        quantize_x(0, 0)
        quantize_x(0, 1)
        copy_bias()
        hidden_passes(0, 0)
        quantize_x(1, 0)
        sort_x(2, 0)
        quantize_x(1, 1)
        sort_x(2, 1)
        hidden_passes(1, 0, 0, 2)
        transpose_x(2, 0)
        transpose_x(2, 1)
        hidden_passes(1, 0, 2, 4)
        for part in range(2):
            sort_x(3, part)
            transpose_x(3, part)
        quantize_x(2, 0)
        quantize_x(2, 1)
        hidden_passes(2, 0)
        sort_x(0, 2)
        sort_x(1, 2)
        quantize_x(3, 0)
        transpose_x(0, 2)
        transpose_x(1, 2)
        for m in (2, 3):
            sort_x(m, 2)
            transpose_x(m, 2)
        quantize_x(3, 1)
        hidden_passes(3, 0)
        quantize_x(0, 2)
        quantize_x(1, 2)
        interleave_ve(0, 0, scalar_cols=0)
        quantize_x(2, 2)
        quantize_ve(0, 0)
        quantize_x(3, 2)
        for m in range(M_TILES):
            hidden_passes(m, 1)
        interleave_ve(0, 1, scalar_cols=192)
        interleave_ve(1, 0, scalar_cols=256)
        quantize_ve(0, 1)
        split_ve(1, 1)
        quantize_ve(1, 0)
        quantize_ve(1, 1)
        for g in range(E_PASSES):
            for m in range(M_TILES):
                emb_passes(m, 0, (g,))
        for m in range(M_TILES):
            emb_passes(m, 1)
        for n in range(3):
            for m in range(M_TILES):
                add_bias(m, n)
            split_ve(n + 2, 0)
            split_ve(n + 2, 1)
            for m in range(M_TILES):
                squash(m, n)
            quantize_ve(n + 2, 0)
            quantize_ve(n + 2, 1)
            if n < 2:
                finish(0, 2, n)
                finish(2, 4, n)
            if n < 2:
                for m in range(M_TILES):
                    hidden_passes(m, n + 2)
                for m in range(M_TILES):
                    emb_passes(m, n + 2)
        finish(0, 2, 2, on_scalar=True)
        finish(2, 4, 2, on_scalar=True)
        for m in range(M_TILES):
            add_bias(m, 3)
            squash(m, 3)
        n = N_TILES - 1
        for m in range(M_TILES):
            hidden_passes(m, n)
            emb_passes(m, n)
        finish(0, 2, 3)
        add_bias(0, n)
        finish(2, 4, 3)
        squash(0, n)
        for m in (1, 2):
            add_bias(m, n)
            squash(m, n)
            finish(m - 1, m, n)
        finish(2, 3, n, on_scalar=True)
        m = M_TILES - 1
        half = N_TILE // 2
        for c0 in (0, half):
            add_bias(m, n, c0, c0 + half)
            squash(m, n, c0, c0 + half)
        for c0 in (0, half):
            finish(m, m + 1, n, c0, c0 + half)
